import numpy as np
import ml_dtypes


def mxq(x, axis, fmt="e4m3"):
    dtype, down = {"e4m3": (ml_dtypes.float8_e4m3fn, 7), "e5m2": (ml_dtypes.float8_e5m2, 14)}[fmt]
    v = np.moveaxis(np.asarray(x, np.float32).astype(ml_dtypes.bfloat16).astype(np.float64), axis, -1)
    blocks = v.reshape(v.shape[:-1] + (-1, 32))
    amax = np.abs(blocks).max(-1, keepdims=True)
    byte = np.maximum(np.where(amax > 0, np.frexp(amax)[1] - 1 + 127, 0) - down, 1)
    scale = np.exp2(byte - 127.0)
    codes = (blocks / scale).astype(np.float32).astype(dtype).astype(np.float64)
    return np.moveaxis((codes * scale).reshape(v.shape), -1, axis)


WIDE = False


def mx_kscale(k):
    if not WIDE:
        return np.ones(k)
    levels = np.array([10, -10, 5, -5, 0])
    if k % 512:
        return np.exp2(np.random.permutation(np.resize(levels, k // 32))).repeat(32)
    a = np.empty((k // 512, 16))
    for p in range(k // 512):
        a[p, :8] = np.random.permutation(np.resize(levels, 8))
        for g in range(8):
            far = levels[np.abs(levels - a[p, g]) >= 10]
            a[p, g + 8] = far[np.random.randint(len(far))]
    return np.exp2(a.ravel()).repeat(32)


BF16 = ml_dtypes.bfloat16


def bf(x):
    return np.asarray(x, np.float32).astype(BF16)


def f64(x):
    return np.asarray(x).astype(np.float64)


E2M1 = np.array([0.0, 0.5, 1.0, 1.5, 2.0, 3.0, 4.0, 6.0, -0.0, -0.5, -1.0, -1.5, -2.0, -3.0, -4.0, -6.0])


def pack_weight(w, fmt):
    k, n = w.shape
    w = f64(bf(w)).reshape(k // 32, 32, n)
    amax = np.abs(w).max(1)
    if fmt == "e4m3":
        byte = np.frexp(amax)[1] - 1 + 127 - 7
    else:
        mant, ex = np.frexp(amax / 6.0)
        byte = np.where(mant > 0.5, ex, ex - 1) + 127
    byte = np.clip(np.where(amax > 0, byte, 1), 1, 254)
    scaled = (w * np.exp2(127.0 - byte)[:, None, :]).reshape(k, n).astype(np.float32)
    by_word = np.ascontiguousarray(scaled.reshape(k // 512, 128, 4, n).transpose(0, 1, 3, 2))
    if fmt == "e4m3":
        words = by_word.astype(ml_dtypes.float8_e4m3fn).view(np.uint8)
    else:
        c = by_word.astype(ml_dtypes.float4_e2m1fn).view(np.uint8) & 0xF
        words = c[..., 0::2] | (c[..., 1::2] << 4)
    return np.ascontiguousarray(words), np.ascontiguousarray(byte.astype(np.uint8).reshape(k // 512, 16, n))


def unpack_weight(words, scales, fmt):
    g, p, n, _ = words.shape
    if fmt == "e4m3":
        vals = np.ascontiguousarray(words).view(ml_dtypes.float8_e4m3fn).astype(np.float64)
    else:
        nib = np.empty((g, p, n, 4), np.uint8)
        nib[..., 0::2] = words & 0xF
        nib[..., 1::2] = words >> 4
        vals = E2M1[nib]
    vals = vals * np.repeat(np.exp2(scales.astype(np.float64) - 127.0), 8, axis=1)[..., None]
    return vals.transpose(0, 1, 3, 2).reshape(g * 512, n)
def pack4(w):
    words, scales = pack_weight(w, "e2m1")
    return words.reshape(words.shape[0], 128, -1), scales


def unpack4(words, scales):
    return unpack_weight(words.reshape(words.shape[0], 128, -1, 2), scales, "e2m1")


E4M3FN = np.array([(-1.0 if i & 128 else 1.0) * ((1.0 + (i & 7) / 8.0) * 2.0 ** (((i >> 3) & 15) - 7) if i & 120 else (i & 7) * 2.0 ** -9) for i in range(256)])


def e4m3fn_bytes(y):
    return np.clip(np.asarray(y, np.float64), -448.0, 448.0).astype(np.float32).astype(ml_dtypes.float8_e4m3fn).view(np.uint8)


def e4m3fn_values(b):
    return E4M3FN[b]


N, D, F, O, T = 1024, 1024, 1024, 512, 3


def normalized_hermite(u):
    u2 = u * u
    u3 = u2 * u
    h1 = u
    h2 = (u2 - 1.0) / np.sqrt(2.0)
    h3 = (u3 - 3.0 * u) / np.sqrt(6.0)
    return h1, h2, h3


def draw0():
    s = mx_kscale(D)
    t = np.stack([mx_kscale(F) for _ in range(T)])
    x = bf(np.random.standard_normal((N, D)) * s)
    words, scales = pack4(np.random.standard_normal((D, F)) / np.sqrt(D) / s[:, None])
    return {"x": x,
            "w_words": words,
            "w_scales": scales,
            "g": bf((1.0 + 0.1 * np.random.standard_normal((T, F))) * t),
            "c": bf(np.random.standard_normal((T, F, O)) / np.sqrt(F) / t[:, :, None]),
            "b": bf(np.random.standard_normal(O) * 0.5)}


def core(x, w_words, w_scales, g, c, b):
    g, c = f64(g), f64(c)
    u = mxq(f64(x), 1, "e4m3") @ unpack4(w_words, w_scales)
    h1, h2, h3 = normalized_hermite(u)
    k1 = h1 * g[0]
    k2 = h2 * g[1]
    k3 = h3 * g[2]
    y1 = mxq(k1, 1, "e4m3") @ mxq(c[0], 0, "e4m3")
    y2 = mxq(k2, 1, "e4m3") @ mxq(c[1], 0, "e4m3")
    y3 = mxq(k3, 1, "e4m3") @ mxq(c[2], 0, "e4m3")
    return y1 + y2 + y3 + f64(b)


def setup_inputs():
    drawn = draw0()
    full = np.asarray(drawn['x']).astype(np.float64)
    scale = (np.abs(full).reshape(1024, 8, 128).max(axis=(2,)) / 448.0).astype(np.float32)
    given = {}
    for key, value in drawn.items():
        if key == 'x':
            given['x_bytes'] = e4m3fn_bytes(full / np.repeat(scale.astype(np.float64), 128, axis=1))
            given['x_scale'] = scale
        else:
            given[key] = value
    return given


def reference(x_bytes, x_scale, w_words, w_scales, g, c, b):
    return core(e4m3fn_values(x_bytes) * np.repeat(x_scale.astype(np.float64), 128, axis=1), w_words, w_scales, g, c, b)

@@ -1,0 +1,332 @@
+from contextlib import ExitStack
+
+import concourse.mybir as mybir
+from concourse.masks import make_identity
+
+N, D, F, O, T = 1024, 1024, 1024, 512, 3
+FLOPS = 2 * N * D * F + T * 2 * N * F * O
+
+F32 = mybir.dt.float32
+BF16 = mybir.dt.bfloat16
+I32 = mybir.dt.int32
+U32 = mybir.dt.uint32
+U8 = mybir.dt.uint8
+FP8 = mybir.dt.float8_e4m3fn
+FP8X4 = mybir.dt.float8_e4m3fn_x4
+FP4X4 = mybir.dt.float4_e2m1fn_x4
+ALU = mybir.AluOpType
+ACT = mybir.ActivationFunctionType
+
+P = 128
+TILES = N // P
+KB = D // 128
+
+X_CHUNKS = ((0, 1), (1, 2), (2, 4), (4, 8))
+C_EARLY = (0,)
+C_STEP = {0: (1,), 1: (2,), 2: (3,), 3: (4,), 4: (5,)}
+READOUT_STEP = {5: (0, 1, 2), 6: (3, 4), 7: (5, 6)}
+
+
+def tile_hermitechaosridgeexpansiondegreethree_d1p_kernel(tc, x_bytes, x_scale, w_words, w_scales, g, c, b, out):
+    nc = tc.nc
+    with ExitStack() as ctx:
+        keep = ctx.enter_context(tc.tile_pool(name="keep", bufs=1))
+        stage = ctx.enter_context(tc.tile_pool(name="stage", bufs=2))
+        psum = ctx.enter_context(tc.psum_pool(name="psum", bufs=2))
+        ctx.enter_context(tc.manual_schedule())
+
+        ws_raw = keep.tile([P, 2, F], U8, name="ws_raw", align_bytes=64)
+        nc.vector.memset(ws_raw[:].rearrange("p g f -> p (g f)").bitcast(I32), 0)
+        g_rows = keep.tile([P, 512], F32, name="g_rows")
+        nc.vector.memset(g_rows[:], 0.0)
+        ident = keep.tile([P, P], F32, name="ident")
+        make_identity(nc, ident[:])
+
+        xs = keep.tile([P, TILES, KB], F32, name="xs")
+        nc.scalar.dma_start(out=xs[:], in_=x_scale.rearrange("(p i) j -> p i j", i=TILES))
+        g_raw = keep.tile([6, 512], BF16, name="g_raw")
+        nc.scalar.dma_start(out=g_raw[:], in_=g.rearrange("d (h f) -> (d h) f", h=2))
+        for q in range(4):
+            nc.scalar.dma_start(
+                out=ws_raw[32 * q : 32 * q + 4, :, :].bitcast(I32),
+                in_=w_scales[:, 4 * q : 4 * q + 4, :].rearrange("g r f -> r g f").bitcast(I32),
+            )
+
+        x_view = x_bytes.rearrange("(p i) k -> p i k", i=TILES)
+        x_codes = {}
+
+        def load_x(n):
+            lo, hi = X_CHUNKS[n]
+            codes = keep.tile([P, hi - lo, D], U8, name="x_codes%d" % n)
+            nc.sync.dma_start(out=codes[:], in_=x_view[:, lo:hi, :])
+            for i in range(lo, hi):
+                x_codes[i] = codes[:, i - lo, :]
+
+        w_raw = {}
+
+        def load_w(h):
+            w_raw[h] = keep.tile([P, 2, 1024], U8, name="w_raw%d" % h)
+            nc.sync.dma_start(
+                out=w_raw[h][:].bitcast(I32),
+                in_=w_words.rearrange("g p f -> p g f")[:, :, 1024 * h : 1024 * (h + 1)].bitcast(I32),
+            )
+
+        c_raw = {}
+
+        def load_c(n):
+            d, h = divmod(n, 2)
+            c_raw[n] = keep.tile([P, 4, O], BF16, name="c_raw%d" % n)
+            rows = c[d, 512 * h : 512 * (h + 1), :].rearrange("(a t r) n -> r a t n", t=4, r=4)
+            for r in range(4):
+                nc.sync.dma_start(out=c_raw[n][r:P:4, :, :], in_=rows[r])
+
+        load_x(0)
+        load_w(0)
+        load_x(1)
+        load_w(1)
+        load_x(2)
+        load_c(0)
+        load_c(1)
+        load_x(3)
+        for n in range(2, 6):
+            load_c(n)
+        bias = keep.tile([P, O], BF16, name="bias")
+        nc.sync.dma_start(out=bias[:], in_=b.partition_broadcast(P))
+
+        xw, xt, xg, xc, xcs = {}, {}, {}, {}, {}
+
+        def widen(i, j, on_vector):
+            if j == 0:
+                xw[i] = stage.tile([P, D], BF16, name="xw", bufs=4, align_bytes=64)
+            cols = slice(128 * j, 128 * (j + 1))
+            codes = x_codes[i][:, cols].bitcast(FP8)
+            if on_vector:
+                nc.vector.tensor_scalar(out=xw[i][:, cols], in0=codes, scalar1=xs[:, i, j : j + 1], scalar2=None, op0=ALU.mult)
+            else:
+                nc.scalar.activation(out=xw[i][:, cols], in_=codes, func=ACT.Copy, scale=xs[:, i, j : j + 1])
+
+        def turn(i):
+            xt[i] = psum.tile([P, 2, 2, P], F32, name="xt", bufs=2)
+            words = xw[i][:].bitcast(F32)
+            for gk in range(2):
+                for u in range(2):
+                    nc.tensor.transpose(xt[i][:, gk, u, :], words[:, 256 * gk + u : 256 * (gk + 1) : 2], ident[:])
+
+        def empty_turned(i):
+            xg[i] = stage.tile([P, 2, P, 4], BF16, name="xg", bufs=3, align_bytes=64)
+            nc.scalar.copy(out=xg[i][:].bitcast(F32), in_=xt[i][:].rearrange("p g u r -> p g r u"))
+
+        def quantize_x(i):
+            xc[i] = stage.tile([P, 2 * P], U32, name="xc", bufs=3, align_bytes=64)
+            xcs[i] = stage.tile([P, 2 * P], U8, name="xcs", bufs=3, align_bytes=64)
+            nc.vector.quantize_mx(out=xc[i][:].bitcast(FP8X4), scales=xcs[i][:], in_=xg[i][:].rearrange("p g r t -> p (g r t)"))
+
+        w_perm = keep.tile([P, 2, 2, 4, 256], U8, name="w_perm", align_bytes=64)
+        ws_perm = keep.tile([P, 2, 2, 4, 128], U8, name="ws_perm", align_bytes=64)
+
+        def permute_w(h):
+            for gk in range(2):
+                nc.vector.tensor_copy(
+                    out=w_perm[:, gk, h, :, :].rearrange("p t b -> p (t b)").bitcast(I32).rearrange("p (t a r) -> p t a r", t=4, r=2),
+                    in_=w_raw[h][:, gk, :].bitcast(I32).rearrange("p (a t r) -> p t a r", t=4, r=2),
+                )
+
+        def permute_ws():
+            nc.vector.tensor_copy(
+                out=ws_perm[:].rearrange("p g h t b -> p (g h t b)").bitcast(I32).rearrange("p (q t a) -> p q t a", q=4, t=4),
+                in_=ws_raw[:].rearrange("p g f -> p (g f)").bitcast(I32).rearrange("p (q a t) -> p q t a", q=4, t=4),
+            )
+
+        g_turned = psum.tile([P, 4, P], F32, name="xt", bufs=2)
+        gains = keep.tile([P, T, 2, 4], F32, name="gains")
+        gain3_bias = keep.tile([P, 2, 4], F32, name="gain3_bias")
+
+        def spread_gains():
+            nc.vector.tensor_copy(
+                out=g_rows[0:6, :].rearrange("p (t a r) -> p t a r", t=4, r=4),
+                in_=g_raw[:].rearrange("p (a t r) -> p t a r", t=4, r=4),
+            )
+
+        def turn_gains():
+            for t in range(4):
+                nc.tensor.transpose(g_turned[:, t, :], g_rows[:, 128 * t : 128 * (t + 1)], ident[:])
+
+        def scale_gains():
+            for d, factor in enumerate((1.0, 2.0**-0.5, 6.0**-0.5)):
+                nc.vector.tensor_scalar(
+                    out=gains[:, d, :, :],
+                    in0=g_turned[:, :, 2 * d : 2 * d + 2].rearrange("p t h -> p h t"),
+                    scalar1=factor,
+                    scalar2=None,
+                    op0=ALU.mult,
+                )
+            nc.vector.tensor_scalar(out=gain3_bias[:], in0=gains[:, 2, :, :], scalar1=-3.0, scalar2=None, op0=ALU.mult)
+
+        u, s, w3 = {}, {}, {}
+        k, kq, ks = {}, {}, {}
+
+        def project(i, h):
+            u[i, h] = psum.tile([P, 4, P], F32, name="u", bufs=4)
+            for t in range(4):
+                for gk in range(2):
+                    nc.tensor.matmul_mx(
+                        out=u[i, h][:, t, :],
+                        lhsT=w_perm[:, gk, h, t, :].bitcast(FP4X4),
+                        lhsT_scale=ws_perm[:, gk, h, t, :],
+                        rhs=xc[i][:, P * gk : P * (gk + 1)].bitcast(FP8X4),
+                        rhs_scale=xcs[i][:, P * gk : P * (gk + 1)],
+                        start=(gk == 0),
+                        stop=(gk == 1),
+                    )
+
+        def square(i, h):
+            s[i, h] = stage.tile([P, 4, P], F32, name="s", bufs=4)
+            nc.scalar.activation(out=s[i, h][:], in_=u[i, h][:], func=ACT.Square)
+
+        def cubic_factor(i, h):
+            w3[i, h] = stage.tile([P, 4, P], F32, name="w3", bufs=4)
+            for t in range(4):
+                nc.scalar.activation(
+                    out=w3[i, h][:, t, :],
+                    in_=s[i, h][:, t, :],
+                    func=ACT.Identity,
+                    scale=gains[:, 2, h, t : t + 1],
+                    bias=gain3_bias[:, h, t : t + 1],
+                )
+
+        def feature_tile(i, d):
+            if (i, d) not in k:
+                k[i, d] = stage.tile([P, 2, P, 4], BF16, name="k%d" % d, bufs=2, align_bytes=64)
+            return k[i, d]
+
+        def by_token(ap):
+            return ap.rearrange("p t r -> p r t")
+
+        def gain_all(d, h):
+            return gains[:, d, h, :].unsqueeze(1).to_broadcast([P, P, 4])
+
+        def feature1(i, h):
+            dst = feature_tile(i, 0)
+            nc.vector.tensor_tensor(out=dst[:, h, :, :], in0=by_token(u[i, h][:]), in1=gain_all(0, h), op=ALU.mult)
+
+        def feature2(i, h):
+            dst = feature_tile(i, 1)
+            nc.vector.scalar_tensor_tensor(
+                out=dst[:, h, :, :], in0=by_token(s[i, h][:]), scalar=-1.0, in1=gain_all(1, h), op0=ALU.add, op1=ALU.mult
+            )
+
+        def feature3(i, h):
+            dst = feature_tile(i, 2)
+            nc.vector.tensor_tensor(out=dst[:, h, :, :], in0=by_token(w3[i, h][:]), in1=by_token(u[i, h][:]), op=ALU.mult)
+
+        def quantize_k(i, d, halves=(0, 2)):
+            if (i, d) not in kq:
+                kq[i, d] = stage.tile([P, 2 * P], U32, name="kq%d" % d, bufs=8, align_bytes=64)
+                ks[i, d] = stage.tile([P, 2 * P], U8, name="ks%d" % d, bufs=8, align_bytes=64)
+            lo, hi = halves
+            cols = slice(P * lo, P * hi)
+            nc.vector.quantize_mx(
+                out=kq[i, d][:, cols].bitcast(FP8X4),
+                scales=ks[i, d][:, cols],
+                in_=k[i, d][:, lo:hi, :, :].rearrange("p h r t -> p (h r t)"),
+            )
+
+        ci, cq, cs, y = {}, {}, {}, {}
+
+        def interleave_c(n, on_vector):
+            ci[n] = stage.tile([P, O, 4], BF16, name="ci", bufs=3, align_bytes=64)
+            dst = ci[n][:].rearrange("p (c i) t -> p c t i", i=4)
+            src = c_raw[n][:].rearrange("p t (c i) -> p c t i", i=4)
+            if on_vector:
+                nc.vector.tensor_copy(out=dst, in_=src)
+            else:
+                nc.scalar.copy(out=dst, in_=src)
+
+        def quantize_c(n):
+            cq[n] = keep.tile([P, O], U32, name="cq%d" % n, align_bytes=64)
+            cs[n] = keep.tile([P, O], U8, name="cs%d" % n, align_bytes=64)
+            nc.vector.quantize_mx(out=cq[n][:].bitcast(FP8X4), scales=cs[n][:], in_=ci[n][:].rearrange("p n t -> p (n t)"))
+
+        def readout(i):
+            y[i] = psum.tile([P, O], F32, name="y", bufs=2)
+            for n in range(6):
+                d, h = divmod(n, 2)
+                cols = slice(P * h, P * (h + 1))
+                nc.tensor.matmul_mx(
+                    out=y[i][:],
+                    lhsT=kq[i, d][:, cols].bitcast(FP8X4),
+                    lhsT_scale=ks[i, d][:, cols],
+                    rhs=cq[n][:].bitcast(FP8X4),
+                    rhs_scale=cs[n][:],
+                    start=(n == 0),
+                    stop=(n == 5),
+                )
+
+        out_view = out.rearrange("(p i) o -> p i o", i=TILES)
+
+        def finish(i):
+            result = stage.tile([P, O], F32, name="result", bufs=3)
+            nc.vector.tensor_tensor(out=result[:], in0=y[i][:], in1=bias[:], op=ALU.add)
+            nc.sync.dma_start(out=out_view[:, i, :], in_=result[:])
+
+        for j in range(KB):
+            widen(0, j, on_vector=(j < 4))
+        spread_gains()
+        turn(0)
+        empty_turned(0)
+        turn_gains()
+        permute_w(0)
+        permute_ws()
+        for j in range(KB):
+            widen(1, j, on_vector=True)
+        turn(1)
+        quantize_x(0)
+        empty_turned(1)
+        project(0, 0)
+        scale_gains()
+        permute_w(1)
+        project(0, 1)
+        for j in range(KB):
+            widen(2, j, on_vector=True)
+        for n in C_EARLY:
+            interleave_c(n, on_vector=True)
+
+        pending_c = list(C_EARLY)
+        for i in range(TILES):
+            square(i, 0)
+            feature1(i, 1)
+            square(i, 1)
+            if i > 0:
+                quantize_k(i - 1, 2)
+            if i + 1 < TILES:
+                quantize_x(i + 1)
+            feature1(i, 0)
+            cubic_factor(i, 0)
+            if i + 2 < TILES:
+                turn(i + 2)
+            if i + 1 < TILES:
+                project(i + 1, 0)
+                project(i + 1, 1)
+            for n in pending_c:
+                quantize_c(n)
+            feature2(i, 0)
+            cubic_factor(i, 1)
+            quantize_k(i, 0)
+            feature2(i, 1)
+            if i + 2 < TILES:
+                empty_turned(i + 2)
+            feature3(i, 0)
+            quantize_k(i, 1)
+            if i + 3 < TILES:
+                for j in range(KB):
+                    widen(i + 3, j, on_vector=False)
+            feature3(i, 1)
+            for m in READOUT_STEP.get(i, ()):
+                readout(m)
+                finish(m)
+            pending_c = list(C_STEP.get(i, ()))
+            for n in pending_c:
+                interleave_c(n, on_vector=False)
+        quantize_k(TILES - 1, 2)
+        readout(TILES - 1)
+        finish(TILES - 1)

@@ -18,13 +18,45 @@ ALU = mybir.AluOpType
 ACT = mybir.ActivationFunctionType
 
 P = 128
+PACK = 4
+KP = D // (P * PACK)
+FH = F // (P * PACK)
 TILES = N // P
+HALVES = 2
+PER_HALF = TILES // HALVES
+TOK = PER_HALF * P
 KB = D // 128
+RUN = 4
 
-X_CHUNKS = ((0, 1), (1, 2), (2, 4), (4, 8))
-C_EARLY = (0,)
-C_STEP = {0: (1,), 1: (2,), 2: (3,), 3: (4,), 4: (5,)}
-READOUT_STEP = {5: (0, 1, 2), 6: (3, 4), 7: (5, 6)}
+GROUPS = tuple((m, h) for m in range(HALVES) for h in range(FH))
+PASSES = tuple((d, h) for h in range(FH) for d in range(T))
+
+X_LOADS = ((0, 1), (1, 2), (2, 4), (4, 8))
+U_BANKS, M_BANKS = 5, 3
+
+TAIL = ((0, 256), (256, 512))
+
+WIDEN_ON_VECTOR = (4, 4, 0, 2, 6, 2, 2, 4)
+EMPTY_ON_VECTOR = (1, 6, 7)
+GAIN2_ON_SCALAR = (0, 0, 0, 4)
+GAIN3_ON_SCALAR = (1, 3, 0, 3)
+INTERLEAVE_ON_SCALAR = (
+    ((0, 0), (1, 0)),
+    ((1, 0), (2, 0)),
+    ((2, 0),),
+    ((0, 0), (0, 256), (1, 256), (2, 256)),
+)
+C_ON_VECTOR = (0, 1, 2, 5)
+
+WIDEN_STEP = (0, 1, 3, 3)
+TURN_DELAY, EMPTY_DELAY = 1, 2
+QUANTIZE_X_STEP = 5
+C_STEP = (0, 2, 3, 7, 8, 9)
+INTERLEAVE_SLOT = (0, 1, 1)
+QUANTIZE_SLOT = 2
+READ_STEP, FINISH_STEP = (10, 10, 11, 12), (12, 12, 14, 16)
+READ_EARLY_STEP = (15, 16, 18, 19)
+CLOSE_STEP, FINISH_LAST_STEP = (16, 20), (18, 20)
 
 
 def tile_hermitechaosridgeexpansiondegreethree_d1p_kernel(tc, x_bytes, x_scale, w_words, w_scales, g, c, b, out):
@@ -33,30 +65,33 @@ def tile_hermitechaosridgeexpansiondegreethree_d1p_kernel(tc, x_bytes, x_scale, 
         keep = ctx.enter_context(tc.tile_pool(name="keep", bufs=1))
         stage = ctx.enter_context(tc.tile_pool(name="stage", bufs=2))
         psum = ctx.enter_context(tc.psum_pool(name="psum", bufs=2))
-        ctx.enter_context(tc.manual_schedule())
 
-        ws_raw = keep.tile([P, 2, F], U8, name="ws_raw", align_bytes=64)
+        ws_raw = keep.tile([P, KP, F], U8, name="ws_raw", align_bytes=64)
         nc.vector.memset(ws_raw[:].rearrange("p g f -> p (g f)").bitcast(I32), 0)
         g_rows = keep.tile([P, 512], F32, name="g_rows")
         nc.vector.memset(g_rows[:], 0.0)
         ident = keep.tile([P, P], F32, name="ident")
         make_identity(nc, ident[:])
+        ident_bf16 = keep.tile([P, P], BF16, name="ident_bf16")
+        nc.vector.tensor_copy(out=ident_bf16[:], in_=ident[:])
 
         xs = keep.tile([P, TILES, KB], F32, name="xs")
         nc.scalar.dma_start(out=xs[:], in_=x_scale.rearrange("(p i) j -> p i j", i=TILES))
-        g_raw = keep.tile([6, 512], BF16, name="g_raw")
-        nc.scalar.dma_start(out=g_raw[:], in_=g.rearrange("d (h f) -> (d h) f", h=2))
-        for q in range(4):
-            nc.scalar.dma_start(
-                out=ws_raw[32 * q : 32 * q + 4, :, :].bitcast(I32),
-                in_=w_scales[:, 4 * q : 4 * q + 4, :].rearrange("g r f -> r g f").bitcast(I32),
-            )
+        g_raw = keep.tile([T * FH, 512], BF16, name="g_raw")
+        nc.scalar.dma_start(out=g_raw[:], in_=g.rearrange("d (h f) -> (d h) f", h=FH))
+
+        def load_w_scales():
+            for q in range(4):
+                nc.sync.dma_start(
+                    out=ws_raw[32 * q : 32 * q + 4, :, :].bitcast(I32),
+                    in_=w_scales[:, 4 * q : 4 * q + 4, :].rearrange("g r f -> r g f").bitcast(I32),
+                )
 
         x_view = x_bytes.rearrange("(p i) k -> p i k", i=TILES)
         x_codes = {}
 
         def load_x(n):
-            lo, hi = X_CHUNKS[n]
+            lo, hi = X_LOADS[n]
             codes = keep.tile([P, hi - lo, D], U8, name="x_codes%d" % n)
             nc.sync.dma_start(out=codes[:], in_=x_view[:, lo:hi, :])
             for i in range(lo, hi):
@@ -65,7 +100,7 @@ def tile_hermitechaosridgeexpansiondegreethree_d1p_kernel(tc, x_bytes, x_scale, 
         w_raw = {}
 
         def load_w(h):
-            w_raw[h] = keep.tile([P, 2, 1024], U8, name="w_raw%d" % h)
+            w_raw[h] = keep.tile([P, KP, 1024], U8, name="w_raw%d" % h)
             nc.sync.dma_start(
                 out=w_raw[h][:].bitcast(I32),
                 in_=w_words.rearrange("g p f -> p g f")[:, :, 1024 * h : 1024 * (h + 1)].bitcast(I32),
@@ -74,192 +109,229 @@ def tile_hermitechaosridgeexpansiondegreethree_d1p_kernel(tc, x_bytes, x_scale, 
         c_raw = {}
 
         def load_c(n):
-            d, h = divmod(n, 2)
-            c_raw[n] = keep.tile([P, 4, O], BF16, name="c_raw%d" % n)
-            rows = c[d, 512 * h : 512 * (h + 1), :].rearrange("(a t r) n -> r a t n", t=4, r=4)
-            for r in range(4):
-                nc.sync.dma_start(out=c_raw[n][r:P:4, :, :], in_=rows[r])
+            d, h = divmod(n, FH)
+            c_raw[n] = keep.tile([P, PACK, O], BF16, name="c_raw%d" % n)
+            rows = c[d, 512 * h : 512 * (h + 1), :].rearrange("(a t r) n -> r a t n", t=PACK, r=RUN)
+            for r in range(RUN):
+                nc.sync.dma_start(out=c_raw[n][r:P:RUN, :, :], in_=rows[r])
 
         load_x(0)
-        load_w(0)
         load_x(1)
-        load_w(1)
+        load_w_scales()
         load_x(2)
+        for h in range(FH):
+            load_w(h)
         load_c(0)
-        load_c(1)
         load_x(3)
-        for n in range(2, 6):
+        for n in range(1, T * FH):
             load_c(n)
         bias = keep.tile([P, O], BF16, name="bias")
         nc.sync.dma_start(out=bias[:], in_=b.partition_broadcast(P))
 
         xw, xt, xg, xc, xcs = {}, {}, {}, {}, {}
 
-        def widen(i, j, on_vector):
-            if j == 0:
-                xw[i] = stage.tile([P, D], BF16, name="xw", bufs=4, align_bytes=64)
-            cols = slice(128 * j, 128 * (j + 1))
-            codes = x_codes[i][:, cols].bitcast(FP8)
-            if on_vector:
-                nc.vector.tensor_scalar(out=xw[i][:, cols], in0=codes, scalar1=xs[:, i, j : j + 1], scalar2=None, op0=ALU.mult)
-            else:
-                nc.scalar.activation(out=xw[i][:, cols], in_=codes, func=ACT.Copy, scale=xs[:, i, j : j + 1])
+        def widen(i):
+            xw[i] = stage.tile([P, D], BF16, name="xw", bufs=5, align_bytes=64)
+            for j in range(KB):
+                cols = slice(128 * j, 128 * (j + 1))
+                codes = x_codes[i][:, cols].bitcast(FP8)
+                scale = xs[:, i, j : j + 1]
+                if j < WIDEN_ON_VECTOR[i]:
+                    nc.vector.tensor_scalar(out=xw[i][:, cols], in0=codes, scalar1=scale, scalar2=None, op0=ALU.mult)
+                else:
+                    nc.scalar.activation(out=xw[i][:, cols], in_=codes, func=ACT.Copy, scale=scale)
 
         def turn(i):
-            xt[i] = psum.tile([P, 2, 2, P], F32, name="xt", bufs=2)
+            xt[i] = psum.tile([P, KP, 2, P], F32, name="m", bufs=M_BANKS)
             words = xw[i][:].bitcast(F32)
-            for gk in range(2):
-                for u in range(2):
-                    nc.tensor.transpose(xt[i][:, gk, u, :], words[:, 256 * gk + u : 256 * (gk + 1) : 2], ident[:])
+            for gk in range(KP):
+                for v in range(2):
+                    nc.tensor.transpose(xt[i][:, gk, v, :], words[:, 256 * gk + v : 256 * (gk + 1) : 2], ident[:])
 
         def empty_turned(i):
-            xg[i] = stage.tile([P, 2, P, 4], BF16, name="xg", bufs=3, align_bytes=64)
-            nc.scalar.copy(out=xg[i][:].bitcast(F32), in_=xt[i][:].rearrange("p g u r -> p g r u"))
+            m, a = divmod(i, PER_HALF)
+            if m not in xg:
+                xg[m] = stage.tile([P, KP, TOK, PACK], BF16, name="xg", bufs=2, align_bytes=64)
+            dst = xg[m][:, :, P * a : P * (a + 1), :].bitcast(F32)
+            src = xt[i][:].rearrange("p g v r -> p g r v")
+            if i in EMPTY_ON_VECTOR:
+                nc.vector.tensor_copy(out=dst, in_=src)
+            else:
+                nc.scalar.copy(out=dst, in_=src)
 
-        def quantize_x(i):
-            xc[i] = stage.tile([P, 2 * P], U32, name="xc", bufs=3, align_bytes=64)
-            xcs[i] = stage.tile([P, 2 * P], U8, name="xcs", bufs=3, align_bytes=64)
-            nc.vector.quantize_mx(out=xc[i][:].bitcast(FP8X4), scales=xcs[i][:], in_=xg[i][:].rearrange("p g r t -> p (g r t)"))
-
-        w_perm = keep.tile([P, 2, 2, 4, 256], U8, name="w_perm", align_bytes=64)
-        ws_perm = keep.tile([P, 2, 2, 4, 128], U8, name="ws_perm", align_bytes=64)
-
-        def permute_w(h):
-            for gk in range(2):
-                nc.vector.tensor_copy(
-                    out=w_perm[:, gk, h, :, :].rearrange("p t b -> p (t b)").bitcast(I32).rearrange("p (t a r) -> p t a r", t=4, r=2),
-                    in_=w_raw[h][:, gk, :].bitcast(I32).rearrange("p (a t r) -> p t a r", t=4, r=2),
-                )
-
-        def permute_ws():
-            nc.vector.tensor_copy(
-                out=ws_perm[:].rearrange("p g h t b -> p (g h t b)").bitcast(I32).rearrange("p (q t a) -> p q t a", q=4, t=4),
-                in_=ws_raw[:].rearrange("p g f -> p (g f)").bitcast(I32).rearrange("p (q a t) -> p q t a", q=4, t=4),
+        def quantize_x(m, gk, lo, hi):
+            if m not in xc:
+                xc[m] = stage.tile([P, KP, TOK], U32, name="xc", bufs=2, align_bytes=64)
+                xcs[m] = stage.tile([P, KP, TOK], U8, name="xcs", bufs=2, align_bytes=64)
+            nc.vector.quantize_mx(
+                out=xc[m][:, gk, lo:hi].bitcast(FP8X4),
+                scales=xcs[m][:, gk, lo:hi],
+                in_=xg[m][:, gk, lo:hi, :].rearrange("p r t -> p (r t)"),
             )
 
-        g_turned = psum.tile([P, 4, P], F32, name="xt", bufs=2)
-        gains = keep.tile([P, T, 2, 4], F32, name="gains")
-        gain3_bias = keep.tile([P, 2, 4], F32, name="gain3_bias")
+        w_perm = keep.tile([P, KP, FH, PACK, 256], U8, name="w_perm", align_bytes=64)
+        ws_perm = keep.tile([P, KP, FH, PACK, 128], U8, name="ws_perm", align_bytes=64)
+
+        def permute_w(h):
+            for gk in range(KP):
+                dst = w_perm[:, gk, h, :, :].rearrange("p t b -> p (t b)").bitcast(I32)
+                src = w_raw[h][:, gk, :].bitcast(I32)
+                nc.vector.tensor_copy(
+                    out=dst.rearrange("p (t a r) -> p t a r", t=PACK, r=2),
+                    in_=src.rearrange("p (a t r) -> p t a r", t=PACK, r=2),
+                )
+
+        def permute_w_scales():
+            dst = ws_perm[:].rearrange("p g h t b -> p (g h t b)").bitcast(I32)
+            src = ws_raw[:].rearrange("p g f -> p (g f)").bitcast(I32)
+            nc.vector.tensor_copy(
+                out=dst.rearrange("p (q t a) -> p q t a", q=KP * FH, t=PACK),
+                in_=src.rearrange("p (q a t) -> p q t a", q=KP * FH, t=PACK),
+            )
+
+        gains = keep.tile([P, T, FH, PACK], F32, name="gains")
+        gain2_bias = keep.tile([P, FH, PACK], F32, name="gain2_bias")
+        gain3_bias = keep.tile([P, FH, PACK], F32, name="gain3_bias")
 
         def spread_gains():
             nc.vector.tensor_copy(
-                out=g_rows[0:6, :].rearrange("p (t a r) -> p t a r", t=4, r=4),
-                in_=g_raw[:].rearrange("p (a t r) -> p t a r", t=4, r=4),
+                out=g_rows[0 : T * FH, :].rearrange("p (t a r) -> p t a r", t=PACK, r=RUN),
+                in_=g_raw[:].rearrange("p (a t r) -> p t a r", t=PACK, r=RUN),
             )
 
         def turn_gains():
-            for t in range(4):
+            g_turned = psum.tile([P, PACK, P], F32, name="m", bufs=M_BANKS)
+            for t in range(PACK):
                 nc.tensor.transpose(g_turned[:, t, :], g_rows[:, 128 * t : 128 * (t + 1)], ident[:])
-
-        def scale_gains():
             for d, factor in enumerate((1.0, 2.0**-0.5, 6.0**-0.5)):
                 nc.vector.tensor_scalar(
                     out=gains[:, d, :, :],
-                    in0=g_turned[:, :, 2 * d : 2 * d + 2].rearrange("p t h -> p h t"),
+                    in0=g_turned[:, :, FH * d : FH * (d + 1)].rearrange("p t h -> p h t"),
                     scalar1=factor,
                     scalar2=None,
                     op0=ALU.mult,
                 )
+            nc.vector.tensor_scalar(out=gain2_bias[:], in0=gains[:, 1, :, :], scalar1=-1.0, scalar2=None, op0=ALU.mult)
             nc.vector.tensor_scalar(out=gain3_bias[:], in0=gains[:, 2, :, :], scalar1=-3.0, scalar2=None, op0=ALU.mult)
 
-        u, s, w3 = {}, {}, {}
-        k, kq, ks = {}, {}, {}
+        u, s, factor, features = {}, {}, {}, {}
+        ki, kq, ks = {}, {}, {}
 
-        def project(i, h):
-            u[i, h] = psum.tile([P, 4, P], F32, name="u", bufs=4)
-            for t in range(4):
-                for gk in range(2):
-                    nc.tensor.matmul_mx(
-                        out=u[i, h][:, t, :],
-                        lhsT=w_perm[:, gk, h, t, :].bitcast(FP4X4),
-                        lhsT_scale=ws_perm[:, gk, h, t, :],
-                        rhs=xc[i][:, P * gk : P * (gk + 1)].bitcast(FP8X4),
-                        rhs_scale=xcs[i][:, P * gk : P * (gk + 1)],
-                        start=(gk == 0),
-                        stop=(gk == 1),
-                    )
-
-        def square(i, h):
-            s[i, h] = stage.tile([P, 4, P], F32, name="s", bufs=4)
-            nc.scalar.activation(out=s[i, h][:], in_=u[i, h][:], func=ACT.Square)
-
-        def cubic_factor(i, h):
-            w3[i, h] = stage.tile([P, 4, P], F32, name="w3", bufs=4)
-            for t in range(4):
-                nc.scalar.activation(
-                    out=w3[i, h][:, t, :],
-                    in_=s[i, h][:, t, :],
-                    func=ACT.Identity,
-                    scale=gains[:, 2, h, t : t + 1],
-                    bias=gain3_bias[:, h, t : t + 1],
+        def project(m, h, t):
+            u[m, h, t] = psum.tile([P, TOK], F32, name="u", bufs=U_BANKS)
+            for gk in range(KP):
+                nc.tensor.matmul_mx(
+                    out=u[m, h, t][:],
+                    lhsT=w_perm[:, gk, h, t, :].bitcast(FP4X4),
+                    lhsT_scale=ws_perm[:, gk, h, t, :],
+                    rhs=xc[m][:, gk, :].bitcast(FP8X4),
+                    rhs_scale=xcs[m][:, gk, :],
+                    start=(gk == 0),
+                    stop=(gk == KP - 1),
                 )
 
-        def feature_tile(i, d):
-            if (i, d) not in k:
-                k[i, d] = stage.tile([P, 2, P, 4], BF16, name="k%d" % d, bufs=2, align_bytes=64)
-            return k[i, d]
+        def feature(m, h, d, t, lo, hi):
+            if (m, h, d) not in features:
+                features[m, h, d] = stage.tile([P, PACK, TOK], BF16, name="k%d" % d, bufs=2)
+            return features[m, h, d][:, t, lo:hi]
 
-        def by_token(ap):
-            return ap.rearrange("p t r -> p r t")
+        def shifted_gain(dst, src, shift, gain, gain_bias, on_scalar):
+            if on_scalar:
+                nc.scalar.activation(out=dst, in_=src, func=ACT.Identity, scale=gain, bias=gain_bias)
+            else:
+                nc.vector.tensor_scalar(out=dst, in0=src, scalar1=-shift, scalar2=gain, op0=ALU.add, op1=ALU.mult)
 
-        def gain_all(d, h):
-            return gains[:, d, h, :].unsqueeze(1).to_broadcast([P, P, 4])
+        def gain2(n, t, lo, hi, on_scalar):
+            m, h = GROUPS[n]
+            gain, gain_bias = gains[:, 1, h, t : t + 1], gain2_bias[:, h, t : t + 1]
+            shifted_gain(feature(m, h, 1, t, lo, hi), s[n, t][:, lo:hi], 1.0, gain, gain_bias, on_scalar)
 
-        def feature1(i, h):
-            dst = feature_tile(i, 0)
-            nc.vector.tensor_tensor(out=dst[:, h, :, :], in0=by_token(u[i, h][:]), in1=gain_all(0, h), op=ALU.mult)
+        def gain3(n, t, lo, hi, on_scalar):
+            m, h = GROUPS[n]
+            gain, gain_bias = gains[:, 2, h, t : t + 1], gain3_bias[:, h, t : t + 1]
+            shifted_gain(factor[n, t][:, lo:hi], s[n, t][:, lo:hi], 3.0, gain, gain_bias, on_scalar)
 
-        def feature2(i, h):
-            dst = feature_tile(i, 1)
-            nc.vector.scalar_tensor_tensor(
-                out=dst[:, h, :, :], in0=by_token(s[i, h][:]), scalar=-1.0, in1=gain_all(1, h), op0=ALU.add, op1=ALU.mult
+        def scalar_features(n, t, lo, hi):
+            m, h = GROUPS[n]
+            if (n, t) not in s:
+                s[n, t] = stage.tile([P, TOK], F32, name="s", bufs=5)
+                factor[n, t] = stage.tile([P, TOK], F32, name="factor", bufs=5)
+            bank = u[m, h, t][:, lo:hi]
+            nc.scalar.activation(out=s[n, t][:, lo:hi], in_=bank, func=ACT.Square)
+            nc.scalar.activation(out=feature(m, h, 0, t, lo, hi), in_=bank, func=ACT.Copy, scale=gains[:, 0, h, t : t + 1])
+            if t < GAIN3_ON_SCALAR[n]:
+                gain3(n, t, lo, hi, True)
+            if t < GAIN2_ON_SCALAR[n]:
+                gain2(n, t, lo, hi, True)
+
+        def vector_gains(n, t, lo, hi):
+            if t >= GAIN3_ON_SCALAR[n]:
+                gain3(n, t, lo, hi, False)
+            if t >= GAIN2_ON_SCALAR[n]:
+                gain2(n, t, lo, hi, False)
+
+        def cube(n, t, lo, hi):
+            m, h = GROUPS[n]
+            nc.vector.tensor_tensor(
+                out=feature(m, h, 2, t, lo, hi), in0=factor[n, t][:, lo:hi], in1=u[m, h, t][:, lo:hi], op=ALU.mult
             )
 
-        def feature3(i, h):
-            dst = feature_tile(i, 2)
-            nc.vector.tensor_tensor(out=dst[:, h, :, :], in0=by_token(w3[i, h][:]), in1=by_token(u[i, h][:]), op=ALU.mult)
+        def interleave_views(dst, src):
+            return dst.rearrange("p (c i) t -> p c t i", i=4), src.rearrange("p t (c i) -> p c t i", i=4)
 
-        def quantize_k(i, d, halves=(0, 2)):
-            if (i, d) not in kq:
-                kq[i, d] = stage.tile([P, 2 * P], U32, name="kq%d" % d, bufs=8, align_bytes=64)
-                ks[i, d] = stage.tile([P, 2 * P], U8, name="ks%d" % d, bufs=8, align_bytes=64)
-            lo, hi = halves
-            cols = slice(P * lo, P * hi)
+        def interleave_k(m, h, d, lo=0, hi=TOK):
+            if (m, h, d) not in ki:
+                ki[m, h, d] = stage.tile([P, TOK, PACK], BF16, name="ki", bufs=5, align_bytes=64)
+            dst, src = interleave_views(ki[m, h, d][:, lo:hi, :], features[m, h, d][:, :, lo:hi])
+            if (d, lo) in INTERLEAVE_ON_SCALAR[GROUPS.index((m, h))]:
+                nc.scalar.copy(out=dst, in_=src)
+            else:
+                nc.vector.tensor_copy(out=dst, in_=src)
+
+        def quantize_k(m, h, d, lo=0, hi=TOK):
+            if (m, h, d) not in kq:
+                kq[m, h, d] = keep.tile([P, TOK], U32, name="kq%d%d%d" % (m, h, d), align_bytes=64)
+                ks[m, h, d] = keep.tile([P, TOK], U8, name="ks%d%d%d" % (m, h, d), align_bytes=64)
             nc.vector.quantize_mx(
-                out=kq[i, d][:, cols].bitcast(FP8X4),
-                scales=ks[i, d][:, cols],
-                in_=k[i, d][:, lo:hi, :, :].rearrange("p h r t -> p (h r t)"),
+                out=kq[m, h, d][:, lo:hi].bitcast(FP8X4),
+                scales=ks[m, h, d][:, lo:hi],
+                in_=ki[m, h, d][:, lo:hi, :].rearrange("p r t -> p (r t)"),
             )
 
         ci, cq, cs, y = {}, {}, {}, {}
 
-        def interleave_c(n, on_vector):
-            ci[n] = stage.tile([P, O, 4], BF16, name="ci", bufs=3, align_bytes=64)
-            dst = ci[n][:].rearrange("p (c i) t -> p c t i", i=4)
-            src = c_raw[n][:].rearrange("p t (c i) -> p c t i", i=4)
-            if on_vector:
+        def interleave_c(n):
+            ci[n] = stage.tile([P, O, PACK], BF16, name="ci", bufs=3, align_bytes=64)
+            if n in C_ON_VECTOR:
+                dst, src = interleave_views(ci[n][:], c_raw[n][:])
                 nc.vector.tensor_copy(out=dst, in_=src)
-            else:
-                nc.scalar.copy(out=dst, in_=src)
+                return
+            for start in range(0, O, 256):
+                bank = psum.tile([P, 256, PACK], BF16, name="m", bufs=M_BANKS)
+                for part in range(0, 256, 128):
+                    columns = c_raw[n][:, :, start + part : start + part + 128].rearrange("p t n -> p n t")
+                    nc.tensor.matmul(bank[:, part : part + 128, :], lhsT=ident_bf16[:], rhs=columns, start=True, stop=True)
+                nc.scalar.copy(out=ci[n][:, start : start + 256, :], in_=bank[:])
 
         def quantize_c(n):
             cq[n] = keep.tile([P, O], U32, name="cq%d" % n, align_bytes=64)
             cs[n] = keep.tile([P, O], U8, name="cs%d" % n, align_bytes=64)
             nc.vector.quantize_mx(out=cq[n][:].bitcast(FP8X4), scales=cs[n][:], in_=ci[n][:].rearrange("p n t -> p (n t)"))
 
-        def readout(i):
-            y[i] = psum.tile([P, O], F32, name="y", bufs=2)
-            for n in range(6):
-                d, h = divmod(n, 2)
-                cols = slice(P * h, P * (h + 1))
+        def readout(i, passes):
+            m, a = divmod(i, PER_HALF)
+            cols = slice(P * a, P * (a + 1))
+            if i not in y:
+                y[i] = psum.tile([P, O], F32, name="m", bufs=M_BANKS)
+            for d, h in passes:
                 nc.tensor.matmul_mx(
                     out=y[i][:],
-                    lhsT=kq[i, d][:, cols].bitcast(FP8X4),
-                    lhsT_scale=ks[i, d][:, cols],
-                    rhs=cq[n][:].bitcast(FP8X4),
-                    rhs_scale=cs[n][:],
-                    start=(n == 0),
-                    stop=(n == 5),
+                    lhsT=kq[m, h, d][:, cols].bitcast(FP8X4),
+                    lhsT_scale=ks[m, h, d][:, cols],
+                    rhs=cq[FH * d + h][:].bitcast(FP8X4),
+                    rhs_scale=cs[FH * d + h][:],
+                    start=((d, h) == PASSES[0]),
+                    stop=((d, h) == PASSES[-1]),
                 )
 
         out_view = out.rearrange("(p i) o -> p i o", i=TILES)
@@ -269,64 +341,90 @@ def tile_hermitechaosridgeexpansiondegreethree_d1p_kernel(tc, x_bytes, x_scale, 
             nc.vector.tensor_tensor(out=result[:], in0=y[i][:], in1=bias[:], op=ALU.add)
             nc.sync.dma_start(out=out_view[:, i, :], in_=result[:])
 
-        for j in range(KB):
-            widen(0, j, on_vector=(j < 4))
-        spread_gains()
-        turn(0)
-        empty_turned(0)
-        turn_gains()
-        permute_w(0)
-        permute_ws()
-        for j in range(KB):
-            widen(1, j, on_vector=True)
-        turn(1)
-        quantize_x(0)
-        empty_turned(1)
-        project(0, 0)
-        scale_gains()
+        for i in range(PER_HALF + 2):
+            if i < PER_HALF:
+                widen(i)
+            if i == 1:
+                permute_w_scales()
+            if i == 2:
+                spread_gains()
+                permute_w(0)
+            if 0 < i <= PER_HALF:
+                turn(i - 1)
+                empty_turned(i - 1)
+            if i == 2:
+                turn_gains()
+            if i > 1:
+                for gk in range(KP):
+                    quantize_x(0, gk, P * (i - 2), P * (i - 1))
+        for t in range(PACK):
+            project(0, 0, t)
         permute_w(1)
-        project(0, 1)
-        for j in range(KB):
-            widen(2, j, on_vector=True)
-        for n in C_EARLY:
-            interleave_c(n, on_vector=True)
 
-        pending_c = list(C_EARLY)
-        for i in range(TILES):
-            square(i, 0)
-            feature1(i, 1)
-            square(i, 1)
-            if i > 0:
-                quantize_k(i - 1, 2)
-            if i + 1 < TILES:
-                quantize_x(i + 1)
-            feature1(i, 0)
-            cubic_factor(i, 0)
-            if i + 2 < TILES:
-                turn(i + 2)
-            if i + 1 < TILES:
-                project(i + 1, 0)
-                project(i + 1, 1)
-            for n in pending_c:
-                quantize_c(n)
-            feature2(i, 0)
-            cubic_factor(i, 1)
-            quantize_k(i, 0)
-            feature2(i, 1)
-            if i + 2 < TILES:
-                empty_turned(i + 2)
-            feature3(i, 0)
-            quantize_k(i, 1)
-            if i + 3 < TILES:
-                for j in range(KB):
-                    widen(i + 3, j, on_vector=False)
-            feature3(i, 1)
-            for m in READOUT_STEP.get(i, ()):
-                readout(m)
-                finish(m)
-            pending_c = list(C_STEP.get(i, ()))
-            for n in pending_c:
-                interleave_c(n, on_vector=False)
-        quantize_k(TILES - 1, 2)
-        readout(TILES - 1)
-        finish(TILES - 1)
+        steps = [(n, t, 0, TOK) for n in range(len(GROUPS) - 1) for t in range(PACK)]
+        tail_tiles = [range(PER_HALF + lo // P, PER_HALF + hi // P) for lo, hi in TAIL]
+        first_tail_step = len(steps)
+        steps += [(len(GROUPS) - 1, t, lo, hi) for lo, hi in TAIL for t in range(PACK)]
+        unprojected = []
+        for step in range(len(steps) + 1):
+            group, slot = divmod(step, PACK)
+            complete = GROUPS[group - 1] if 0 < group < len(GROUPS) else None
+            if step < len(steps):
+                scalar_features(*steps[step])
+            if step > 0:
+                vector_gains(*steps[step - 1])
+            if complete:
+                for d in range(T):
+                    if slot == INTERLEAVE_SLOT[d]:
+                        interleave_k(*complete, d)
+            for a in range(PER_HALF):
+                if step == WIDEN_STEP[a]:
+                    widen(PER_HALF + a)
+                if step == WIDEN_STEP[a] + TURN_DELAY:
+                    turn(PER_HALF + a)
+                if step == WIDEN_STEP[a] + EMPTY_DELAY:
+                    empty_turned(PER_HALF + a)
+            for n in range(T * FH):
+                if step == C_STEP[n]:
+                    interleave_c(n)
+            if step > 0:
+                cube(*steps[step - 1])
+            if step == QUANTIZE_X_STEP:
+                for gk in range(KP):
+                    quantize_x(1, gk, 0, TOK)
+            if complete and slot == QUANTIZE_SLOT:
+                for d in range(T):
+                    quantize_k(*complete, d)
+            for n in range(T * FH):
+                if step == C_STEP[n] + 1:
+                    quantize_c(n)
+            if step < first_tail_step:
+                m, h = GROUPS[group + 1]
+                unprojected.append((m, h, slot))
+                if m in xc:
+                    for waiting in unprojected:
+                        project(*waiting)
+                    unprojected.clear()
+            for i in range(PER_HALF):
+                if step == FINISH_STEP[i]:
+                    finish(i)
+                if step == READ_STEP[i]:
+                    readout(i, PASSES)
+            for a in range(PER_HALF):
+                if step == READ_EARLY_STEP[a]:
+                    readout(PER_HALF + a, PASSES[:T])
+            m, h = GROUPS[-1]
+            for (lo, hi), tiles, close_step, finish_step in zip(TAIL, tail_tiles, CLOSE_STEP, FINISH_LAST_STEP):
+                if step == close_step:
+                    for d in range(T):
+                        interleave_k(m, h, d, lo, hi)
+                        if d > 0:
+                            quantize_k(m, h, d - 1, lo, hi)
+                            for i in tiles:
+                                readout(i, PASSES[T + d - 1 : T + d])
+                    quantize_k(m, h, T - 1, lo, hi)
+                    for i in tiles:
+                        readout(i, PASSES[-1:])
+                if step == finish_step:
+                    for i in tiles:
+                        finish(i)

from contextlib import ExitStack

import concourse.mybir as mybir
from concourse.masks import make_identity

N, D, F, O, T = 1024, 1024, 1024, 512, 3
FLOPS = 2 * N * D * F + T * 2 * N * F * O

F32 = mybir.dt.float32
BF16 = mybir.dt.bfloat16
I32 = mybir.dt.int32
U32 = mybir.dt.uint32
U8 = mybir.dt.uint8
FP8 = mybir.dt.float8_e4m3fn
FP8X4 = mybir.dt.float8_e4m3fn_x4
FP4X4 = mybir.dt.float4_e2m1fn_x4
ALU = mybir.AluOpType
ACT = mybir.ActivationFunctionType

P = 128
PACK = 4
KP = D // (P * PACK)
FH = F // (P * PACK)
TILES = N // P
HALVES = 2
PER_HALF = TILES // HALVES
TOK = PER_HALF * P
KB = D // 128
RUN = 4

GROUPS = tuple((m, h) for m in range(HALVES) for h in range(FH))
PASSES = tuple((d, h) for h in range(FH) for d in range(T))

X_LOADS = ((0, 1), (1, 2), (2, 4), (4, 8))
U_BANKS, M_BANKS = 5, 3

TAIL = ((0, 256), (256, 512))

WIDEN_ON_VECTOR = (4, 4, 0, 2, 6, 2, 2, 4)
EMPTY_ON_VECTOR = (1, 6, 7)
GAIN2_ON_SCALAR = (0, 0, 0, 4)
GAIN3_ON_SCALAR = (1, 3, 0, 3)
INTERLEAVE_ON_SCALAR = (
    ((0, 0), (1, 0)),
    ((1, 0), (2, 0)),
    ((2, 0),),
    ((0, 0), (0, 256), (1, 256), (2, 256)),
)
C_ON_VECTOR = (0, 1, 2, 5)

WIDEN_STEP = (0, 1, 3, 3)
TURN_DELAY, EMPTY_DELAY = 1, 2
QUANTIZE_X_STEP = 5
C_STEP = (0, 2, 3, 7, 8, 9)
INTERLEAVE_SLOT = (0, 1, 1)
QUANTIZE_SLOT = 2
READ_STEP, FINISH_STEP = (10, 10, 11, 12), (12, 12, 14, 16)
READ_EARLY_STEP = (15, 16, 18, 19)
CLOSE_STEP, FINISH_LAST_STEP = (16, 20), (18, 20)


def tile_hermitechaosridgeexpansiondegreethree_d1p_kernel(tc, x_bytes, x_scale, w_words, w_scales, g, c, b, out):
    nc = tc.nc
    with ExitStack() as ctx:
        keep = ctx.enter_context(tc.tile_pool(name="keep", bufs=1))
        stage = ctx.enter_context(tc.tile_pool(name="stage", bufs=2))
        psum = ctx.enter_context(tc.psum_pool(name="psum", bufs=2))

        ws_raw = keep.tile([P, KP, F], U8, name="ws_raw", align_bytes=64)
        nc.vector.memset(ws_raw[:].rearrange("p g f -> p (g f)").bitcast(I32), 0)
        g_rows = keep.tile([P, 512], F32, name="g_rows")
        nc.vector.memset(g_rows[:], 0.0)
        ident = keep.tile([P, P], F32, name="ident")
        make_identity(nc, ident[:])
        ident_bf16 = keep.tile([P, P], BF16, name="ident_bf16")
        nc.vector.tensor_copy(out=ident_bf16[:], in_=ident[:])

        xs = keep.tile([P, TILES, KB], F32, name="xs")
        nc.scalar.dma_start(out=xs[:], in_=x_scale.rearrange("(p i) j -> p i j", i=TILES))
        g_raw = keep.tile([T * FH, 512], BF16, name="g_raw")
        nc.scalar.dma_start(out=g_raw[:], in_=g.rearrange("d (h f) -> (d h) f", h=FH))

        def load_w_scales():
            for q in range(4):
                nc.sync.dma_start(
                    out=ws_raw[32 * q : 32 * q + 4, :, :].bitcast(I32),
                    in_=w_scales[:, 4 * q : 4 * q + 4, :].rearrange("g r f -> r g f").bitcast(I32),
                )

        x_view = x_bytes.rearrange("(p i) k -> p i k", i=TILES)
        x_codes = {}

        def load_x(n):
            lo, hi = X_LOADS[n]
            codes = keep.tile([P, hi - lo, D], U8, name="x_codes%d" % n)
            nc.sync.dma_start(out=codes[:], in_=x_view[:, lo:hi, :])
            for i in range(lo, hi):
                x_codes[i] = codes[:, i - lo, :]

        w_raw = {}

        def load_w(h):
            w_raw[h] = keep.tile([P, KP, 1024], U8, name="w_raw%d" % h)
            nc.sync.dma_start(
                out=w_raw[h][:].bitcast(I32),
                in_=w_words.rearrange("g p f -> p g f")[:, :, 1024 * h : 1024 * (h + 1)].bitcast(I32),
            )

        c_raw = {}

        def load_c(n):
            d, h = divmod(n, FH)
            c_raw[n] = keep.tile([P, PACK, O], BF16, name="c_raw%d" % n)
            rows = c[d, 512 * h : 512 * (h + 1), :].rearrange("(a t r) n -> r a t n", t=PACK, r=RUN)
            for r in range(RUN):
                nc.sync.dma_start(out=c_raw[n][r:P:RUN, :, :], in_=rows[r])

        load_x(0)
        load_x(1)
        load_w_scales()
        load_x(2)
        for h in range(FH):
            load_w(h)
        load_c(0)
        load_x(3)
        for n in range(1, T * FH):
            load_c(n)
        bias = keep.tile([P, O], BF16, name="bias")
        nc.sync.dma_start(out=bias[:], in_=b.partition_broadcast(P))

        xw, xt, xg, xc, xcs = {}, {}, {}, {}, {}

        def widen(i):
            xw[i] = stage.tile([P, D], BF16, name="xw", bufs=5, align_bytes=64)
            for j in range(KB):
                cols = slice(128 * j, 128 * (j + 1))
                codes = x_codes[i][:, cols].bitcast(FP8)
                scale = xs[:, i, j : j + 1]
                if j < WIDEN_ON_VECTOR[i]:
                    nc.vector.tensor_scalar(out=xw[i][:, cols], in0=codes, scalar1=scale, scalar2=None, op0=ALU.mult)
                else:
                    nc.scalar.activation(out=xw[i][:, cols], in_=codes, func=ACT.Copy, scale=scale)

        def turn(i):
            xt[i] = psum.tile([P, KP, 2, P], F32, name="m", bufs=M_BANKS)
            words = xw[i][:].bitcast(F32)
            for gk in range(KP):
                for v in range(2):
                    nc.tensor.transpose(xt[i][:, gk, v, :], words[:, 256 * gk + v : 256 * (gk + 1) : 2], ident[:])

        def empty_turned(i):
            m, a = divmod(i, PER_HALF)
            if m not in xg:
                xg[m] = stage.tile([P, KP, TOK, PACK], BF16, name="xg", bufs=2, align_bytes=64)
            dst = xg[m][:, :, P * a : P * (a + 1), :].bitcast(F32)
            src = xt[i][:].rearrange("p g v r -> p g r v")
            if i in EMPTY_ON_VECTOR:
                nc.vector.tensor_copy(out=dst, in_=src)
            else:
                nc.scalar.copy(out=dst, in_=src)

        def quantize_x(m, gk, lo, hi):
            if m not in xc:
                xc[m] = stage.tile([P, KP, TOK], U32, name="xc", bufs=2, align_bytes=64)
                xcs[m] = stage.tile([P, KP, TOK], U8, name="xcs", bufs=2, align_bytes=64)
            nc.vector.quantize_mx(
                out=xc[m][:, gk, lo:hi].bitcast(FP8X4),
                scales=xcs[m][:, gk, lo:hi],
                in_=xg[m][:, gk, lo:hi, :].rearrange("p r t -> p (r t)"),
            )

        w_perm = keep.tile([P, KP, FH, PACK, 256], U8, name="w_perm", align_bytes=64)
        ws_perm = keep.tile([P, KP, FH, PACK, 128], U8, name="ws_perm", align_bytes=64)

        def permute_w(h):
            for gk in range(KP):
                dst = w_perm[:, gk, h, :, :].rearrange("p t b -> p (t b)").bitcast(I32)
                src = w_raw[h][:, gk, :].bitcast(I32)
                nc.vector.tensor_copy(
                    out=dst.rearrange("p (t a r) -> p t a r", t=PACK, r=2),
                    in_=src.rearrange("p (a t r) -> p t a r", t=PACK, r=2),
                )

        def permute_w_scales():
            dst = ws_perm[:].rearrange("p g h t b -> p (g h t b)").bitcast(I32)
            src = ws_raw[:].rearrange("p g f -> p (g f)").bitcast(I32)
            nc.vector.tensor_copy(
                out=dst.rearrange("p (q t a) -> p q t a", q=KP * FH, t=PACK),
                in_=src.rearrange("p (q a t) -> p q t a", q=KP * FH, t=PACK),
            )

        gains = keep.tile([P, T, FH, PACK], F32, name="gains")
        gain2_bias = keep.tile([P, FH, PACK], F32, name="gain2_bias")
        gain3_bias = keep.tile([P, FH, PACK], F32, name="gain3_bias")

        def spread_gains():
            nc.vector.tensor_copy(
                out=g_rows[0 : T * FH, :].rearrange("p (t a r) -> p t a r", t=PACK, r=RUN),
                in_=g_raw[:].rearrange("p (a t r) -> p t a r", t=PACK, r=RUN),
            )

        def turn_gains():
            g_turned = psum.tile([P, PACK, P], F32, name="m", bufs=M_BANKS)
            for t in range(PACK):
                nc.tensor.transpose(g_turned[:, t, :], g_rows[:, 128 * t : 128 * (t + 1)], ident[:])
            for d, factor in enumerate((1.0, 2.0**-0.5, 6.0**-0.5)):
                nc.vector.tensor_scalar(
                    out=gains[:, d, :, :],
                    in0=g_turned[:, :, FH * d : FH * (d + 1)].rearrange("p t h -> p h t"),
                    scalar1=factor,
                    scalar2=None,
                    op0=ALU.mult,
                )
            nc.vector.tensor_scalar(out=gain2_bias[:], in0=gains[:, 1, :, :], scalar1=-1.0, scalar2=None, op0=ALU.mult)
            nc.vector.tensor_scalar(out=gain3_bias[:], in0=gains[:, 2, :, :], scalar1=-3.0, scalar2=None, op0=ALU.mult)

        u, s, factor, features = {}, {}, {}, {}
        ki, kq, ks = {}, {}, {}

        def project(m, h, t):
            u[m, h, t] = psum.tile([P, TOK], F32, name="u", bufs=U_BANKS)
            for gk in range(KP):
                nc.tensor.matmul_mx(
                    out=u[m, h, t][:],
                    lhsT=w_perm[:, gk, h, t, :].bitcast(FP4X4),
                    lhsT_scale=ws_perm[:, gk, h, t, :],
                    rhs=xc[m][:, gk, :].bitcast(FP8X4),
                    rhs_scale=xcs[m][:, gk, :],
                    start=(gk == 0),
                    stop=(gk == KP - 1),
                )

        def feature(m, h, d, t, lo, hi):
            if (m, h, d) not in features:
                features[m, h, d] = stage.tile([P, PACK, TOK], BF16, name="k%d" % d, bufs=2)
            return features[m, h, d][:, t, lo:hi]

        def shifted_gain(dst, src, shift, gain, gain_bias, on_scalar):
            if on_scalar:
                nc.scalar.activation(out=dst, in_=src, func=ACT.Identity, scale=gain, bias=gain_bias)
            else:
                nc.vector.tensor_scalar(out=dst, in0=src, scalar1=-shift, scalar2=gain, op0=ALU.add, op1=ALU.mult)

        def gain2(n, t, lo, hi, on_scalar):
            m, h = GROUPS[n]
            gain, gain_bias = gains[:, 1, h, t : t + 1], gain2_bias[:, h, t : t + 1]
            shifted_gain(feature(m, h, 1, t, lo, hi), s[n, t][:, lo:hi], 1.0, gain, gain_bias, on_scalar)

        def gain3(n, t, lo, hi, on_scalar):
            m, h = GROUPS[n]
            gain, gain_bias = gains[:, 2, h, t : t + 1], gain3_bias[:, h, t : t + 1]
            shifted_gain(factor[n, t][:, lo:hi], s[n, t][:, lo:hi], 3.0, gain, gain_bias, on_scalar)

        def scalar_features(n, t, lo, hi):
            m, h = GROUPS[n]
            if (n, t) not in s:
                s[n, t] = stage.tile([P, TOK], F32, name="s", bufs=5)
                factor[n, t] = stage.tile([P, TOK], F32, name="factor", bufs=5)
            bank = u[m, h, t][:, lo:hi]
            nc.scalar.activation(out=s[n, t][:, lo:hi], in_=bank, func=ACT.Square)
            nc.scalar.activation(out=feature(m, h, 0, t, lo, hi), in_=bank, func=ACT.Copy, scale=gains[:, 0, h, t : t + 1])
            if t < GAIN3_ON_SCALAR[n]:
                gain3(n, t, lo, hi, True)
            if t < GAIN2_ON_SCALAR[n]:
                gain2(n, t, lo, hi, True)

        def vector_gains(n, t, lo, hi):
            if t >= GAIN3_ON_SCALAR[n]:
                gain3(n, t, lo, hi, False)
            if t >= GAIN2_ON_SCALAR[n]:
                gain2(n, t, lo, hi, False)

        def cube(n, t, lo, hi):
            m, h = GROUPS[n]
            nc.vector.tensor_tensor(
                out=feature(m, h, 2, t, lo, hi), in0=factor[n, t][:, lo:hi], in1=u[m, h, t][:, lo:hi], op=ALU.mult
            )

        def interleave_views(dst, src):
            return dst.rearrange("p (c i) t -> p c t i", i=4), src.rearrange("p t (c i) -> p c t i", i=4)

        def interleave_k(m, h, d, lo=0, hi=TOK):
            if (m, h, d) not in ki:
                ki[m, h, d] = stage.tile([P, TOK, PACK], BF16, name="ki", bufs=5, align_bytes=64)
            dst, src = interleave_views(ki[m, h, d][:, lo:hi, :], features[m, h, d][:, :, lo:hi])
            if (d, lo) in INTERLEAVE_ON_SCALAR[GROUPS.index((m, h))]:
                nc.scalar.copy(out=dst, in_=src)
            else:
                nc.vector.tensor_copy(out=dst, in_=src)

        def quantize_k(m, h, d, lo=0, hi=TOK):
            if (m, h, d) not in kq:
                kq[m, h, d] = keep.tile([P, TOK], U32, name="kq%d%d%d" % (m, h, d), align_bytes=64)
                ks[m, h, d] = keep.tile([P, TOK], U8, name="ks%d%d%d" % (m, h, d), align_bytes=64)
            nc.vector.quantize_mx(
                out=kq[m, h, d][:, lo:hi].bitcast(FP8X4),
                scales=ks[m, h, d][:, lo:hi],
                in_=ki[m, h, d][:, lo:hi, :].rearrange("p r t -> p (r t)"),
            )

        ci, cq, cs, y = {}, {}, {}, {}

        def interleave_c(n):
            ci[n] = stage.tile([P, O, PACK], BF16, name="ci", bufs=3, align_bytes=64)
            if n in C_ON_VECTOR:
                dst, src = interleave_views(ci[n][:], c_raw[n][:])
                nc.vector.tensor_copy(out=dst, in_=src)
                return
            for start in range(0, O, 256):
                bank = psum.tile([P, 256, PACK], BF16, name="m", bufs=M_BANKS)
                for part in range(0, 256, 128):
                    columns = c_raw[n][:, :, start + part : start + part + 128].rearrange("p t n -> p n t")
                    nc.tensor.matmul(bank[:, part : part + 128, :], lhsT=ident_bf16[:], rhs=columns, start=True, stop=True)
                nc.scalar.copy(out=ci[n][:, start : start + 256, :], in_=bank[:])

        def quantize_c(n):
            cq[n] = keep.tile([P, O], U32, name="cq%d" % n, align_bytes=64)
            cs[n] = keep.tile([P, O], U8, name="cs%d" % n, align_bytes=64)
            nc.vector.quantize_mx(out=cq[n][:].bitcast(FP8X4), scales=cs[n][:], in_=ci[n][:].rearrange("p n t -> p (n t)"))

        def readout(i, passes):
            m, a = divmod(i, PER_HALF)
            cols = slice(P * a, P * (a + 1))
            if i not in y:
                y[i] = psum.tile([P, O], F32, name="m", bufs=M_BANKS)
            for d, h in passes:
                nc.tensor.matmul_mx(
                    out=y[i][:],
                    lhsT=kq[m, h, d][:, cols].bitcast(FP8X4),
                    lhsT_scale=ks[m, h, d][:, cols],
                    rhs=cq[FH * d + h][:].bitcast(FP8X4),
                    rhs_scale=cs[FH * d + h][:],
                    start=((d, h) == PASSES[0]),
                    stop=((d, h) == PASSES[-1]),
                )

        out_view = out.rearrange("(p i) o -> p i o", i=TILES)

        def finish(i):
            result = stage.tile([P, O], F32, name="result", bufs=3)
            nc.vector.tensor_tensor(out=result[:], in0=y[i][:], in1=bias[:], op=ALU.add)
            nc.sync.dma_start(out=out_view[:, i, :], in_=result[:])

        for i in range(PER_HALF + 2):
            if i < PER_HALF:
                widen(i)
            if i == 1:
                permute_w_scales()
            if i == 2:
                spread_gains()
                permute_w(0)
            if 0 < i <= PER_HALF:
                turn(i - 1)
                empty_turned(i - 1)
            if i == 2:
                turn_gains()
            if i > 1:
                for gk in range(KP):
                    quantize_x(0, gk, P * (i - 2), P * (i - 1))
        for t in range(PACK):
            project(0, 0, t)
        permute_w(1)

        steps = [(n, t, 0, TOK) for n in range(len(GROUPS) - 1) for t in range(PACK)]
        tail_tiles = [range(PER_HALF + lo // P, PER_HALF + hi // P) for lo, hi in TAIL]
        first_tail_step = len(steps)
        steps += [(len(GROUPS) - 1, t, lo, hi) for lo, hi in TAIL for t in range(PACK)]
        unprojected = []
        for step in range(len(steps) + 1):
            group, slot = divmod(step, PACK)
            complete = GROUPS[group - 1] if 0 < group < len(GROUPS) else None
            if step < len(steps):
                scalar_features(*steps[step])
            if step > 0:
                vector_gains(*steps[step - 1])
            if complete:
                for d in range(T):
                    if slot == INTERLEAVE_SLOT[d]:
                        interleave_k(*complete, d)
            for a in range(PER_HALF):
                if step == WIDEN_STEP[a]:
                    widen(PER_HALF + a)
                if step == WIDEN_STEP[a] + TURN_DELAY:
                    turn(PER_HALF + a)
                if step == WIDEN_STEP[a] + EMPTY_DELAY:
                    empty_turned(PER_HALF + a)
            for n in range(T * FH):
                if step == C_STEP[n]:
                    interleave_c(n)
            if step > 0:
                cube(*steps[step - 1])
            if step == QUANTIZE_X_STEP:
                for gk in range(KP):
                    quantize_x(1, gk, 0, TOK)
            if complete and slot == QUANTIZE_SLOT:
                for d in range(T):
                    quantize_k(*complete, d)
            for n in range(T * FH):
                if step == C_STEP[n] + 1:
                    quantize_c(n)
            if step < first_tail_step:
                m, h = GROUPS[group + 1]
                unprojected.append((m, h, slot))
                if m in xc:
                    for waiting in unprojected:
                        project(*waiting)
                    unprojected.clear()
            for i in range(PER_HALF):
                if step == FINISH_STEP[i]:
                    finish(i)
                if step == READ_STEP[i]:
                    readout(i, PASSES)
            for a in range(PER_HALF):
                if step == READ_EARLY_STEP[a]:
                    readout(PER_HALF + a, PASSES[:T])
            m, h = GROUPS[-1]
            for (lo, hi), tiles, close_step, finish_step in zip(TAIL, tail_tiles, CLOSE_STEP, FINISH_LAST_STEP):
                if step == close_step:
                    for d in range(T):
                        interleave_k(m, h, d, lo, hi)
                        if d > 0:
                            quantize_k(m, h, d - 1, lo, hi)
                            for i in tiles:
                                readout(i, PASSES[T + d - 1 : T + d])
                    quantize_k(m, h, T - 1, lo, hi)
                    for i in tiles:
                        readout(i, PASSES[-1:])
                if step == finish_step:
                    for i in tiles:
                        finish(i)
